import numpy as np
import ml_dtypes


def mxq(x, axis, fmt="e4m3"):
    dtype, down = {"e4m3": (ml_dtypes.float8_e4m3fn, 7), "e5m2": (ml_dtypes.float8_e5m2, 14)}[fmt]
    v = np.moveaxis(np.asarray(x, np.float32).astype(ml_dtypes.bfloat16).astype(np.float64), axis, -1)
    blocks = v.reshape(v.shape[:-1] + (-1, 32))
    amax = np.abs(blocks).max(-1, keepdims=True)
    byte = np.maximum(np.where(amax > 0, np.frexp(amax)[1] - 1 + 127, 0) - down, 1)
    scale = np.exp2(byte - 127.0)
    codes = (blocks / scale).astype(np.float32).astype(dtype).astype(np.float64)
    return np.moveaxis((codes * scale).reshape(v.shape), -1, axis)


WIDE = False


def mx_kscale(k):
    if not WIDE:
        return np.ones(k)
    levels = np.array([30, -30])
    if k % 512:
        return np.exp2(np.random.permutation(np.resize(levels, k // 32))).repeat(32)
    a = np.empty((k // 512, 16))
    for p in range(k // 512):
        a[p, :8] = np.random.permutation(np.resize(levels, 8))
        for g in range(8):
            far = levels[np.abs(levels - a[p, g]) >= 10]
            a[p, g + 8] = far[np.random.randint(len(far))]
    return np.exp2(a.ravel()).repeat(32)


def f64(x):
    return np.asarray(x).astype(np.float64)


def striped(idx):
    return np.tile(np.asarray(idx).reshape(-1, 16).T, (8, 1)).astype(np.uint16)


def unstriped(offs):
    return offs[:16].T.reshape(-1).astype(np.int64)


E2M1 = np.array([0.0, 0.5, 1.0, 1.5, 2.0, 3.0, 4.0, 6.0, -0.0, -0.5, -1.0, -1.5, -2.0, -3.0, -4.0, -6.0])


def pack_weight(w, fmt):
    k, n = w.shape
    w = f64(np.asarray(w, np.float32).astype(ml_dtypes.bfloat16)).reshape(k // 32, 32, n)
    amax = np.abs(w).max(1)
    if fmt in ("e4m3", "e5m2"):
        byte = np.frexp(amax)[1] - 1 + 127 - (7 if fmt == "e4m3" else 14)
    else:
        mant, ex = np.frexp(amax / 6.0)
        byte = np.where(mant > 0.5, ex, ex - 1) + 127
    byte = np.clip(np.where(amax > 0, byte, 1), 1, 254)
    scaled = (w * np.exp2(127.0 - byte)[:, None, :]).reshape(k, n).astype(np.float32)
    by_word = np.ascontiguousarray(scaled.reshape(k // 512, 128, 4, n).transpose(0, 1, 3, 2))
    if fmt in ("e4m3", "e5m2"):
        words = by_word.astype(ml_dtypes.float8_e4m3fn if fmt == "e4m3" else ml_dtypes.float8_e5m2).view(np.uint8)
    else:
        c = by_word.astype(ml_dtypes.float4_e2m1fn).view(np.uint8) & 0xF
        words = (c[..., 0::2] | (c[..., 1::2] << 4)).reshape(k // 512, 128, 2 * n)
    return np.ascontiguousarray(words), np.ascontiguousarray(byte.astype(np.uint8).reshape(k // 512, 16, n))


def unpack_weight(words, scales, fmt):
    g, _, n = scales.shape
    words = np.ascontiguousarray(words).reshape(g, 128, n, -1)
    if fmt in ("e4m3", "e5m2"):
        vals = words.view(ml_dtypes.float8_e4m3fn if fmt == "e4m3" else ml_dtypes.float8_e5m2).astype(np.float64)
    else:
        nib = np.empty((g, 128, n, 4), np.uint8)
        nib[..., 0::2] = words & 0xF
        nib[..., 1::2] = words >> 4
        vals = E2M1[nib]
    vals = vals * np.repeat(np.exp2(scales.astype(np.float64) - 127.0), 8, axis=1)[..., None]
    return vals.transpose(0, 1, 3, 2).reshape(g * 512, n)


K, F, T, Z, J, R, O, N, L = 512, 512, 1024, 1024, 256, 512, 128, 256, 512


def setup_inputs():
    n = np.random.standard_normal
    idx = np.random.permutation(T)[:J]
    idx2 = np.random.permutation(Z)[:J]
    idx3 = np.random.permutation(J)[:O]
    idx4 = np.random.permutation(J)[:O]
    fk = mx_kscale(K)
    fr = mx_kscale(R)
    ff = mx_kscale(F)
    fl = mx_kscale(L)
    xtp = pack_weight(n((K, T)) / fk[:, None], "e5m2")
    wp = pack_weight(n((K, R)) * 1 / np.sqrt(K) * fk[:, None] * fr, "e2m1")
    xop = pack_weight(n((F, Z)) / ff[:, None], "e4m3")
    w2p = pack_weight(n((F, R)) * 1 / np.sqrt(F) * ff[:, None] * fr, "e2m1")
    wbp = pack_weight(n((R, N)) * 1 / np.sqrt(R) / fr[:, None], "e2m1")
    sxp = pack_weight(n((L, O)) / fl[:, None], "e4m3")
    wsp = pack_weight(n((L, N)) * 1 / np.sqrt(L) * fl[:, None], "e2m1")
    return {
        "xt_words": xtp[0],
        "xt_scales": xtp[1],
        "w_words": wp[0],
        "w_scales": wp[1],
        "xo_words": xop[0],
        "xo_scales": xop[1],
        "w2_words": w2p[0],
        "w2_scales": w2p[1],
        "wb_words": wbp[0],
        "wb_scales": wbp[1],
        "sx_words": sxp[0],
        "sx_scales": sxp[1],
        "ws_words": wsp[0],
        "ws_scales": wsp[1],
        "offs": striped(idx),
        "offs2": striped(idx2),
        "offs3": striped(idx3),
        "offs4": striped(idx4),
    }


def reference(xt_words, xt_scales, w_words, w_scales, xo_words, xo_scales, w2_words, w2_scales, wb_words, wb_scales, sx_words, sx_scales, ws_words, ws_scales, offs, offs2, offs3, offs4):
    idx = unstriped(offs)
    idx2 = unstriped(offs2)
    idx3 = unstriped(offs3)
    idx4 = unstriped(offs4)
    xtu = unpack_weight(xt_words, xt_scales, "e5m2")
    wu = unpack_weight(w_words, w_scales, "e2m1")
    xou = unpack_weight(xo_words, xo_scales, "e4m3")
    w2u = unpack_weight(w2_words, w2_scales, "e2m1")
    wbu = unpack_weight(wb_words, wb_scales, "e2m1")
    sxu = unpack_weight(sx_words, sx_scales, "e4m3")
    wsu = unpack_weight(ws_words, ws_scales, "e2m1")
    xtidxg = xtu[:, idx]
    a = wu.T @ xtidxg
    xoidx2g = xou[:, idx2]
    b = w2u.T @ xoidx2g
    hid = np.maximum(a[:, idx3], b[:, idx4])
    hidq = mxq(hid, 0, "e4m3")
    y = wbu.T @ hidq + wsu.T @ sxu
    return y

@@ -1,0 +1,169 @@
+from contextlib import ExitStack
+
+import concourse.mybir as mybir
+
+K, T, J, R, O, N = 512, 1024, 256, 512, 128, 256
+FLOPS = 2 * (2 * K * R * J + 2 * R * N * O)
+
+F32 = mybir.dt.float32
+BF16 = mybir.dt.bfloat16
+I32 = mybir.dt.int32
+U32 = mybir.dt.uint32
+U16 = mybir.dt.uint16
+U8 = mybir.dt.uint8
+E4X4 = mybir.dt.float8_e4m3fn_x4
+E5X4 = mybir.dt.float8_e5m2_x4
+E2X4 = mybir.dt.float4_e2m1fn_x4
+COPY = mybir.ActivationFunctionType.Copy
+MAX = mybir.AluOpType.max
+P = 128
+
+
+def tile_list_twotab_looked_skip_plain_kernel(
+    tc, xt_words, xt_scales, w_words, w_scales, xo_words, xo_scales, w2_words, w2_scales,
+    wb_words, wb_scales, sx_words, sx_scales, ws_words, ws_scales, offs, offs2, offs3, offs4, out,
+):
+    nc = tc.nc
+    with ExitStack() as ctx:
+        sb = ctx.enter_context(tc.tile_pool(name="sb", bufs=1))
+        shared = ctx.enter_context(tc.tile_pool(name="shared", bufs=1))
+        ps = ctx.enter_context(tc.psum_pool(name="ps", bufs=1))
+
+        def tile(name, shape, dtype):
+            return sb.tile(shape, dtype, name=name, align_bytes=64)
+
+        def words32(ap):
+            return ap[0].rearrange("p n t -> p (n t)").bitcast(I32)
+
+        l1 = sb.tile([P, J // 16], U16, name="l1")
+        l2 = sb.tile([P, J // 16], U16, name="l2")
+        l3 = sb.tile([P, O // 16], U16, name="l3")
+        l4 = sb.tile([P, O // 16], U16, name="l4")
+        xt_w = tile("xt_w", [P, T], U32)
+        xo_w = tile("xo_w", [P, T], U32)
+        xt_s = tile("xt_s", [P, T], U8)
+        xo_s = tile("xo_s", [P, T], U8)
+        w_w = tile("w_w", [P, 2 * R], U8)
+        w2_w = tile("w2_w", [P, 2 * R], U8)
+        m_s = shared.tile([P, 2 * R], U8, name="m_s", align_bytes=64, offset=2 * J)
+        wb_w = tile("wb_w", [P, 2 * N], U8)
+        ws_w = tile("ws_w", [P, 2 * N], U8)
+        sx_w = tile("sx_w", [P, O], U32)
+        a_s = tile("a_s", [P, R + J], U8)
+        b_s = tile("b_s", [P, R + J + 2 * N + O], U8)
+        wb0 = R + J
+        ws0 = wb0 + N
+        sx0 = ws0 + N
+
+        for plane in (xt_s[:], m_s[:], xo_s[:], b_s[:, wb0:]):
+            nc.vector.memset(plane.bitcast(I32), 0)
+
+        def rows16(queue, dst, scales):
+            queue.dma_start(out=dst.bitcast(I32), in_=scales[0].bitcast(I32))
+
+        def spread(plane):
+            for q in range(1, 4):
+                nc.sync.dma_start(out=plane[32 * q : 32 * q + 4, :].bitcast(I32), in_=plane[4 * q : 4 * q + 4, :].bitcast(I32))
+
+        nc.gpsimd.dma_start(out=xt_w[:].bitcast(I32), in_=words32(xt_words))
+        nc.sync.dma_start(l1[:], offs)
+        rows16(nc.scalar, xt_s[0:16, :], xt_scales)
+        nc.sync.dma_start(out=w_w[:].bitcast(I32), in_=w_words[0].bitcast(I32))
+        rows16(nc.scalar, m_s[0:16, 0:R], w_scales)
+        nc.sync.dma_start(l2[:], offs2)
+        nc.gpsimd.dma_start(out=xo_w[:].bitcast(I32), in_=words32(xo_words))
+        rows16(nc.scalar, xo_s[0:16, :], xo_scales)
+        nc.sync.dma_start(out=w2_w[:].bitcast(I32), in_=w2_words[0].bitcast(I32))
+        rows16(nc.scalar, m_s[0:16, R : 2 * R], w2_scales)
+        nc.sync.dma_start(l3[:], offs3)
+        nc.sync.dma_start(l4[:], offs4)
+        rows16(nc.sync, b_s[0:16, wb0:ws0], wb_scales)
+        rows16(nc.sync, b_s[0:16, ws0:sx0], ws_scales)
+        rows16(nc.sync, b_s[0:16, sx0 : sx0 + O], sx_scales)
+        nc.gpsimd.dma_start(out=wb_w[:].bitcast(I32), in_=wb_words[0].bitcast(I32))
+        nc.gpsimd.dma_start(out=ws_w[:].bitcast(I32), in_=ws_words[0].bitcast(I32))
+        nc.gpsimd.dma_start(out=sx_w[:].bitcast(I32), in_=words32(sx_words))
+
+        def scale_stage(tag, x_s, lst, raw, plane):
+            g_s = tile(tag + "g_s", [P, J], U8)
+            nc.vector.tensor_copy(out=g_s[:], in_=x_s[:].indirect(lst[:]))
+            nc.vector.tensor_copy(
+                out=plane[:, 0:R].rearrange("p (t m) -> p t m", t=4),
+                in_=raw.rearrange("p (m t) -> p t m", t=4),
+            )
+            nc.vector.tensor_copy(out=plane[:, R : R + J].bitcast(I32), in_=g_s[:].bitcast(I32))
+            spread(plane)
+
+        scale_stage("a", xt_s, l1, m_s[:, 0:R], a_s)
+        scale_stage("b", xo_s, l2, m_s[:, R : 2 * R], b_s)
+
+        def first_stage(tag, x_w, lst, x_dtype, m_w, plane, place):
+            g_w = shared.tile([P, J], U32, name=tag + "g_w", align_bytes=64, offset=place)
+            p_w = tile(tag + "p_w", [P, 2 * R], U8)
+            nc.scalar.copy(
+                out=p_w[:].bitcast(U16).rearrange("p (t m) -> p t m", t=4),
+                in_=m_w[:].bitcast(U16).rearrange("p (m t) -> p t m", t=4),
+            )
+            nc.vector.tensor_copy(out=g_w[:], in_=x_w[:].indirect(lst[:]))
+            banks = [ps.tile([P, J], F32, name=tag + "bank%d" % t, tag=tag + "bank%d" % t) for t in range(4)]
+            for t in range(4):
+                nc.tensor.matmul_mx(
+                    out=banks[t][:],
+                    lhsT=p_w[:, 2 * P * t : 2 * P * (t + 1)].bitcast(E2X4),
+                    lhsT_scale=plane[:, P * t : P * (t + 1)],
+                    rhs=g_w[:].bitcast(x_dtype),
+                    rhs_scale=plane[:, R : R + J],
+                    start=True,
+                    stop=True,
+                )
+            return banks
+
+        a_banks = first_stage("a", xt_w, l1, E5X4, w_w, a_s, 0)
+        b_banks = first_stage("b", xo_w, l2, E4X4, w2_w, b_s, 4 * J)
+
+        a_pick = tile("a_pick", [P, 4, O], F32)
+        b_pick = tile("b_pick", [P, 4, O], F32)
+        for tag, banks, pick, lst in (("a", a_banks, a_pick, l3), ("b", b_banks, b_pick, l4)):
+            for t in range(4):
+                whole = tile(tag + "whole%d" % t, [P, J], F32)
+                nc.scalar.copy(out=whole[:], in_=banks[t][:])
+                nc.vector.tensor_copy(out=pick[:, t, :], in_=whole[:].indirect(lst[:]))
+
+        y = [ps.tile([P, O], F32, name="y%d" % h, tag="abank%d" % h) for h in range(2)]
+        for h in range(2):
+            nc.tensor.matmul_mx(
+                out=y[h][:],
+                lhsT=ws_w[:, 2 * P * h : 2 * P * (h + 1)].bitcast(E2X4),
+                lhsT_scale=b_s[:, ws0 + P * h : ws0 + P * (h + 1)],
+                rhs=sx_w[:].bitcast(E4X4),
+                rhs_scale=b_s[:, sx0 : sx0 + O],
+                start=True,
+                stop=False,
+            )
+
+        hid = tile("hid", [P, 4 * O], BF16)
+        nc.vector.tensor_tensor(
+            out=hid[:].rearrange("p (c i t) -> p c t i", i=4, t=4),
+            in0=a_pick[:].rearrange("p t (c i) -> p c t i", i=4),
+            in1=b_pick[:].rearrange("p t (c i) -> p c t i", i=4),
+            op=MAX,
+        )
+        h_w = tile("h_w", [P, O], U32)
+        h_s = tile("h_s", [P, O], U8)
+        nc.vector.quantize_mx(out=h_w[:].bitcast(E4X4), scales=h_s[:], in_=hid[:])
+
+        res = [tile("res%d" % h, [P, O], F32) for h in range(2)]
+        for h in range(2):
+            nc.tensor.matmul_mx(
+                out=y[h][:],
+                lhsT=wb_w[:, 2 * P * h : 2 * P * (h + 1)].bitcast(E2X4),
+                lhsT_scale=b_s[:, wb0 + P * h : wb0 + P * (h + 1)],
+                rhs=h_w[:].bitcast(E4X4),
+                rhs_scale=h_s[:],
+                start=False,
+                stop=True,
+            )
+        nc.vector.tensor_copy(out=res[0][:], in_=y[0][:])
+        nc.scalar.copy(out=res[1][:], in_=y[1][:])
+        nc.sync.dma_start(out=out[0:P, :], in_=res[0][:])
+        nc.scalar.dma_start(out=out[P : 2 * P, :], in_=res[1][:])

@@ -32,73 +32,61 @@ def tile_list_twotab_looked_skip_plain_kernel(
         def tile(name, shape, dtype):
             return sb.tile(shape, dtype, name=name, align_bytes=64)
 
+        def placed(name, shape, dtype, offset):
+            return shared.tile(shape, dtype, name=name, align_bytes=64, offset=offset)
+
         def words32(ap):
             return ap[0].rearrange("p n t -> p (n t)").bitcast(I32)
+
+        def rows16(queue, dst, scales):
+            rows = scales[0].bitcast(I32)
+            queue.dma_start(out=dst.bitcast(I32), in_=rows.unsqueeze(1).to_broadcast([16, 8, rows.shape[1]]))
+
+        def spread(plane, queues):
+            for i in range(1, 4):
+                queues[i - 1].dma_start(out=plane[i:P:32, :].bitcast(I32), in_=plane[8 * i : P : 32, :].bitcast(I32))
 
         l1 = sb.tile([P, J // 16], U16, name="l1")
         l2 = sb.tile([P, J // 16], U16, name="l2")
         l3 = sb.tile([P, O // 16], U16, name="l3")
         l4 = sb.tile([P, O // 16], U16, name="l4")
-        xt_w = tile("xt_w", [P, T], U32)
+        xt_w = placed("xt_w", [P, T], U32, 4096)
         xo_w = tile("xo_w", [P, T], U32)
         xt_s = tile("xt_s", [P, T], U8)
         xo_s = tile("xo_s", [P, T], U8)
         w_w = tile("w_w", [P, 2 * R], U8)
-        w2_w = tile("w2_w", [P, 2 * R], U8)
-        m_s = shared.tile([P, 2 * R], U8, name="m_s", align_bytes=64, offset=2 * J)
-        wb_w = tile("wb_w", [P, 2 * N], U8)
-        ws_w = tile("ws_w", [P, 2 * N], U8)
-        sx_w = tile("sx_w", [P, O], U32)
+        w2_w = placed("w2_w", [P, 2 * R], U8, 2048 + 256)
+        w_s = tile("w_s", [P, R], U8)
+        w2_s = tile("w2_s", [P, R], U8)
         a_s = tile("a_s", [P, R + J], U8)
-        b_s = tile("b_s", [P, R + J + 2 * N + O], U8)
-        wb0 = R + J
-        ws0 = wb0 + N
-        sx0 = ws0 + N
+        b_s = tile("b_s", [P, R + J], U8)
+        ga_s = placed("ga_s", [P, J], U8, 1024 - 128)
+        gb_s = placed("gb_s", [P, J], U8, 1024 - 128)
 
-        for plane in (xt_s[:], m_s[:], xo_s[:], b_s[:, wb0:]):
-            nc.vector.memset(plane.bitcast(I32), 0)
-
-        def rows16(queue, dst, scales):
-            queue.dma_start(out=dst.bitcast(I32), in_=scales[0].bitcast(I32))
-
-        def spread(plane):
-            for q in range(1, 4):
-                nc.sync.dma_start(out=plane[32 * q : 32 * q + 4, :].bitcast(I32), in_=plane[4 * q : 4 * q + 4, :].bitcast(I32))
-
-        nc.gpsimd.dma_start(out=xt_w[:].bitcast(I32), in_=words32(xt_words))
-        nc.sync.dma_start(l1[:], offs)
-        rows16(nc.scalar, xt_s[0:16, :], xt_scales)
-        nc.sync.dma_start(out=w_w[:].bitcast(I32), in_=w_words[0].bitcast(I32))
-        rows16(nc.scalar, m_s[0:16, 0:R], w_scales)
-        nc.sync.dma_start(l2[:], offs2)
+        rows16(nc.sync, w_s[:], w_scales)
+        rows16(nc.scalar, xt_s[:], xt_scales)
         nc.gpsimd.dma_start(out=xo_w[:].bitcast(I32), in_=words32(xo_words))
-        rows16(nc.scalar, xo_s[0:16, :], xo_scales)
-        nc.sync.dma_start(out=w2_w[:].bitcast(I32), in_=w2_words[0].bitcast(I32))
-        rows16(nc.scalar, m_s[0:16, R : 2 * R], w2_scales)
+        nc.sync.dma_start(l1[:], offs)
+        nc.scalar.dma_start(out=w_w[:].bitcast(I32), in_=w_words[0].bitcast(I32))
+        nc.sync.dma_start(l2[:], offs2)
+        rows16(nc.sync, xo_s[:], xo_scales)
+        rows16(nc.scalar, w2_s[:], w2_scales)
+        nc.sync.dma_start(out=xt_w[:].bitcast(I32), in_=words32(xt_words))
+        nc.gpsimd.dma_start(out=w2_w[:].bitcast(I32), in_=w2_words[0].bitcast(I32))
         nc.sync.dma_start(l3[:], offs3)
         nc.sync.dma_start(l4[:], offs4)
-        rows16(nc.sync, b_s[0:16, wb0:ws0], wb_scales)
-        rows16(nc.sync, b_s[0:16, ws0:sx0], ws_scales)
-        rows16(nc.sync, b_s[0:16, sx0 : sx0 + O], sx_scales)
-        nc.gpsimd.dma_start(out=wb_w[:].bitcast(I32), in_=wb_words[0].bitcast(I32))
-        nc.gpsimd.dma_start(out=ws_w[:].bitcast(I32), in_=ws_words[0].bitcast(I32))
-        nc.gpsimd.dma_start(out=sx_w[:].bitcast(I32), in_=words32(sx_words))
 
-        def scale_stage(tag, x_s, lst, raw, plane):
-            g_s = tile(tag + "g_s", [P, J], U8)
+        for x_s, lst, g_s, m_s, plane, queues in ((xt_s, l1, ga_s, w_s, a_s, (nc.sync, nc.scalar, nc.sync)), (xo_s, l2, gb_s, w2_s, b_s, (nc.sync, nc.scalar, nc.sync))):
             nc.vector.tensor_copy(out=g_s[:], in_=x_s[:].indirect(lst[:]))
             nc.vector.tensor_copy(
                 out=plane[:, 0:R].rearrange("p (t m) -> p t m", t=4),
-                in_=raw.rearrange("p (m t) -> p t m", t=4),
+                in_=m_s[:].rearrange("p (m t) -> p t m", t=4),
             )
-            nc.vector.tensor_copy(out=plane[:, R : R + J].bitcast(I32), in_=g_s[:].bitcast(I32))
-            spread(plane)
-
-        scale_stage("a", xt_s, l1, m_s[:, 0:R], a_s)
-        scale_stage("b", xo_s, l2, m_s[:, R : 2 * R], b_s)
+            nc.vector.tensor_copy(out=plane[:, R:].bitcast(I32), in_=g_s[:].bitcast(I32))
+            spread(plane, queues)
 
         def first_stage(tag, x_w, lst, x_dtype, m_w, plane, place):
-            g_w = shared.tile([P, J], U32, name=tag + "g_w", align_bytes=64, offset=place)
+            g_w = placed(tag + "g_w", [P, J], U32, place)
             p_w = tile(tag + "p_w", [P, 2 * R], U8)
             nc.scalar.copy(
                 out=p_w[:].bitcast(U16).rearrange("p (t m) -> p t m", t=4),
@@ -112,42 +100,61 @@ def tile_list_twotab_looked_skip_plain_kernel(
                     lhsT=p_w[:, 2 * P * t : 2 * P * (t + 1)].bitcast(E2X4),
                     lhsT_scale=plane[:, P * t : P * (t + 1)],
                     rhs=g_w[:].bitcast(x_dtype),
-                    rhs_scale=plane[:, R : R + J],
+                    rhs_scale=plane[:, R:],
                     start=True,
                     stop=True,
                 )
             return banks
 
         a_banks = first_stage("a", xt_w, l1, E5X4, w_w, a_s, 0)
-        b_banks = first_stage("b", xo_w, l2, E4X4, w2_w, b_s, 4 * J)
+        b_banks = first_stage("b", xo_w, l2, E4X4, w2_w, b_s, 4096)
+
+        c_s = placed("c_s", [P, 2 * N + O], U8, 1024)
+        wb_w = placed("wb_w", [P, 2 * N], U8, 2048)
+        ws_w = placed("ws_w", [P, 2 * N], U8, 2048 + 512)
+        sx_w = placed("sx_w", [P, O], U32, 2048 + 1024)
+        rows16(nc.sync, c_s[:, 0:N], wb_scales)
+        rows16(nc.sync, c_s[:, N : 2 * N], ws_scales)
+        rows16(nc.sync, c_s[:, 2 * N :], sx_scales)
+        nc.sync.dma_start(out=ws_w[:].bitcast(I32), in_=ws_words[0].bitcast(I32))
+        nc.sync.dma_start(out=sx_w[:].bitcast(I32), in_=words32(sx_words))
+        nc.sync.dma_start(out=wb_w[:].bitcast(I32), in_=wb_words[0].bitcast(I32))
+        spread(c_s, (nc.sync, nc.sync, nc.sync))
 
         a_pick = tile("a_pick", [P, 4, O], F32)
         b_pick = tile("b_pick", [P, 4, O], F32)
         for tag, banks, pick, lst in (("a", a_banks, a_pick, l3), ("b", b_banks, b_pick, l4)):
             for t in range(4):
                 whole = tile(tag + "whole%d" % t, [P, J], F32)
-                nc.scalar.copy(out=whole[:], in_=banks[t][:])
-                nc.vector.tensor_copy(out=pick[:, t, :], in_=whole[:].indirect(lst[:]))
+                if (tag, t) in (("a", 1),):
+                    nc.vector.tensor_copy(out=whole[:], in_=banks[t][:])
+                else:
+                    nc.scalar.copy(out=whole[:], in_=banks[t][:])
+                if (tag, t) in (("b", 3),):
+                    nc.scalar.activation(out=pick[:, t, :], in_=whole[:].indirect(lst[:]), func=COPY)
+                else:
+                    nc.vector.tensor_copy(out=pick[:, t, :], in_=whole[:].indirect(lst[:]))
 
         y = [ps.tile([P, O], F32, name="y%d" % h, tag="abank%d" % h) for h in range(2)]
         for h in range(2):
             nc.tensor.matmul_mx(
                 out=y[h][:],
                 lhsT=ws_w[:, 2 * P * h : 2 * P * (h + 1)].bitcast(E2X4),
-                lhsT_scale=b_s[:, ws0 + P * h : ws0 + P * (h + 1)],
+                lhsT_scale=c_s[:, N + P * h : N + P * (h + 1)],
                 rhs=sx_w[:].bitcast(E4X4),
-                rhs_scale=b_s[:, sx0 : sx0 + O],
+                rhs_scale=c_s[:, 2 * N :],
                 start=True,
                 stop=False,
             )
 
         hid = tile("hid", [P, 4 * O], BF16)
-        nc.vector.tensor_tensor(
-            out=hid[:].rearrange("p (c i t) -> p c t i", i=4, t=4),
-            in0=a_pick[:].rearrange("p t (c i) -> p c t i", i=4),
-            in1=b_pick[:].rearrange("p t (c i) -> p c t i", i=4),
-            op=MAX,
-        )
+        for h in range(2):
+            nc.vector.tensor_tensor(
+                out=hid[:].rearrange("p (c i t) -> p c t i", i=4, t=4)[:, :, 2 * h : 2 * h + 2, :],
+                in0=a_pick[:, 2 * h : 2 * h + 2, :].rearrange("p t (c i) -> p c t i", i=4),
+                in1=b_pick[:, 2 * h : 2 * h + 2, :].rearrange("p t (c i) -> p c t i", i=4),
+                op=MAX,
+            )
         h_w = tile("h_w", [P, O], U32)
         h_s = tile("h_s", [P, O], U8)
         nc.vector.quantize_mx(out=h_w[:].bitcast(E4X4), scales=h_s[:], in_=hid[:])
@@ -157,7 +164,7 @@ def tile_list_twotab_looked_skip_plain_kernel(
             nc.tensor.matmul_mx(
                 out=y[h][:],
                 lhsT=wb_w[:, 2 * P * h : 2 * P * (h + 1)].bitcast(E2X4),
-                lhsT_scale=b_s[:, wb0 + P * h : wb0 + P * (h + 1)],
+                lhsT_scale=c_s[:, P * h : P * (h + 1)],
                 rhs=h_w[:].bitcast(E4X4),
                 rhs_scale=h_s[:],
                 start=False,

from contextlib import ExitStack

import concourse.mybir as mybir

K, T, J, R, O, N = 512, 1024, 256, 512, 128, 256
FLOPS = 2 * (2 * K * R * J + 2 * R * N * O)

F32 = mybir.dt.float32
BF16 = mybir.dt.bfloat16
I32 = mybir.dt.int32
U32 = mybir.dt.uint32
U16 = mybir.dt.uint16
U8 = mybir.dt.uint8
E4X4 = mybir.dt.float8_e4m3fn_x4
E5X4 = mybir.dt.float8_e5m2_x4
E2X4 = mybir.dt.float4_e2m1fn_x4
COPY = mybir.ActivationFunctionType.Copy
MAX = mybir.AluOpType.max
P = 128


def tile_list_twotab_looked_skip_plain_kernel(
    tc, xt_words, xt_scales, w_words, w_scales, xo_words, xo_scales, w2_words, w2_scales,
    wb_words, wb_scales, sx_words, sx_scales, ws_words, ws_scales, offs, offs2, offs3, offs4, out,
):
    nc = tc.nc
    with ExitStack() as ctx:
        sb = ctx.enter_context(tc.tile_pool(name="sb", bufs=1))
        shared = ctx.enter_context(tc.tile_pool(name="shared", bufs=1))
        ps = ctx.enter_context(tc.psum_pool(name="ps", bufs=1))

        def tile(name, shape, dtype):
            return sb.tile(shape, dtype, name=name, align_bytes=64)

        def placed(name, shape, dtype, offset):
            return shared.tile(shape, dtype, name=name, align_bytes=64, offset=offset)

        def words32(ap):
            return ap[0].rearrange("p n t -> p (n t)").bitcast(I32)

        def rows16(queue, dst, scales):
            rows = scales[0].bitcast(I32)
            queue.dma_start(out=dst.bitcast(I32), in_=rows.unsqueeze(1).to_broadcast([16, 8, rows.shape[1]]))

        def spread(plane, queues):
            for i in range(1, 4):
                queues[i - 1].dma_start(out=plane[i:P:32, :].bitcast(I32), in_=plane[8 * i : P : 32, :].bitcast(I32))

        l1 = sb.tile([P, J // 16], U16, name="l1")
        l2 = sb.tile([P, J // 16], U16, name="l2")
        l3 = sb.tile([P, O // 16], U16, name="l3")
        l4 = sb.tile([P, O // 16], U16, name="l4")
        xt_w = placed("xt_w", [P, T], U32, 4096)
        xo_w = tile("xo_w", [P, T], U32)
        xt_s = tile("xt_s", [P, T], U8)
        xo_s = tile("xo_s", [P, T], U8)
        w_w = tile("w_w", [P, 2 * R], U8)
        w2_w = placed("w2_w", [P, 2 * R], U8, 2048 + 256)
        w_s = tile("w_s", [P, R], U8)
        w2_s = tile("w2_s", [P, R], U8)
        a_s = tile("a_s", [P, R + J], U8)
        b_s = tile("b_s", [P, R + J], U8)
        ga_s = placed("ga_s", [P, J], U8, 1024 - 128)
        gb_s = placed("gb_s", [P, J], U8, 1024 - 128)

        rows16(nc.sync, w_s[:], w_scales)
        rows16(nc.scalar, xt_s[:], xt_scales)
        nc.gpsimd.dma_start(out=xo_w[:].bitcast(I32), in_=words32(xo_words))
        nc.sync.dma_start(l1[:], offs)
        nc.scalar.dma_start(out=w_w[:].bitcast(I32), in_=w_words[0].bitcast(I32))
        nc.sync.dma_start(l2[:], offs2)
        rows16(nc.sync, xo_s[:], xo_scales)
        rows16(nc.scalar, w2_s[:], w2_scales)
        nc.sync.dma_start(out=xt_w[:].bitcast(I32), in_=words32(xt_words))
        nc.gpsimd.dma_start(out=w2_w[:].bitcast(I32), in_=w2_words[0].bitcast(I32))
        nc.sync.dma_start(l3[:], offs3)
        nc.sync.dma_start(l4[:], offs4)

        for x_s, lst, g_s, m_s, plane, queues in ((xt_s, l1, ga_s, w_s, a_s, (nc.sync, nc.scalar, nc.sync)), (xo_s, l2, gb_s, w2_s, b_s, (nc.sync, nc.scalar, nc.sync))):
            nc.vector.tensor_copy(out=g_s[:], in_=x_s[:].indirect(lst[:]))
            nc.vector.tensor_copy(
                out=plane[:, 0:R].rearrange("p (t m) -> p t m", t=4),
                in_=m_s[:].rearrange("p (m t) -> p t m", t=4),
            )
            nc.vector.tensor_copy(out=plane[:, R:].bitcast(I32), in_=g_s[:].bitcast(I32))
            spread(plane, queues)

        def first_stage(tag, x_w, lst, x_dtype, m_w, plane, place):
            g_w = placed(tag + "g_w", [P, J], U32, place)
            p_w = tile(tag + "p_w", [P, 2 * R], U8)
            nc.scalar.copy(
                out=p_w[:].bitcast(U16).rearrange("p (t m) -> p t m", t=4),
                in_=m_w[:].bitcast(U16).rearrange("p (m t) -> p t m", t=4),
            )
            nc.vector.tensor_copy(out=g_w[:], in_=x_w[:].indirect(lst[:]))
            banks = [ps.tile([P, J], F32, name=tag + "bank%d" % t, tag=tag + "bank%d" % t) for t in range(4)]
            for t in range(4):
                nc.tensor.matmul_mx(
                    out=banks[t][:],
                    lhsT=p_w[:, 2 * P * t : 2 * P * (t + 1)].bitcast(E2X4),
                    lhsT_scale=plane[:, P * t : P * (t + 1)],
                    rhs=g_w[:].bitcast(x_dtype),
                    rhs_scale=plane[:, R:],
                    start=True,
                    stop=True,
                )
            return banks

        a_banks = first_stage("a", xt_w, l1, E5X4, w_w, a_s, 0)
        b_banks = first_stage("b", xo_w, l2, E4X4, w2_w, b_s, 4096)

        c_s = placed("c_s", [P, 2 * N + O], U8, 1024)
        wb_w = placed("wb_w", [P, 2 * N], U8, 2048)
        ws_w = placed("ws_w", [P, 2 * N], U8, 2048 + 512)
        sx_w = placed("sx_w", [P, O], U32, 2048 + 1024)
        rows16(nc.sync, c_s[:, 0:N], wb_scales)
        rows16(nc.sync, c_s[:, N : 2 * N], ws_scales)
        rows16(nc.sync, c_s[:, 2 * N :], sx_scales)
        nc.sync.dma_start(out=ws_w[:].bitcast(I32), in_=ws_words[0].bitcast(I32))
        nc.sync.dma_start(out=sx_w[:].bitcast(I32), in_=words32(sx_words))
        nc.sync.dma_start(out=wb_w[:].bitcast(I32), in_=wb_words[0].bitcast(I32))
        spread(c_s, (nc.sync, nc.sync, nc.sync))

        a_pick = tile("a_pick", [P, 4, O], F32)
        b_pick = tile("b_pick", [P, 4, O], F32)
        for tag, banks, pick, lst in (("a", a_banks, a_pick, l3), ("b", b_banks, b_pick, l4)):
            for t in range(4):
                whole = tile(tag + "whole%d" % t, [P, J], F32)
                if (tag, t) in (("a", 1),):
                    nc.vector.tensor_copy(out=whole[:], in_=banks[t][:])
                else:
                    nc.scalar.copy(out=whole[:], in_=banks[t][:])
                if (tag, t) in (("b", 3),):
                    nc.scalar.activation(out=pick[:, t, :], in_=whole[:].indirect(lst[:]), func=COPY)
                else:
                    nc.vector.tensor_copy(out=pick[:, t, :], in_=whole[:].indirect(lst[:]))

        y = [ps.tile([P, O], F32, name="y%d" % h, tag="abank%d" % h) for h in range(2)]
        for h in range(2):
            nc.tensor.matmul_mx(
                out=y[h][:],
                lhsT=ws_w[:, 2 * P * h : 2 * P * (h + 1)].bitcast(E2X4),
                lhsT_scale=c_s[:, N + P * h : N + P * (h + 1)],
                rhs=sx_w[:].bitcast(E4X4),
                rhs_scale=c_s[:, 2 * N :],
                start=True,
                stop=False,
            )

        hid = tile("hid", [P, 4 * O], BF16)
        for h in range(2):
            nc.vector.tensor_tensor(
                out=hid[:].rearrange("p (c i t) -> p c t i", i=4, t=4)[:, :, 2 * h : 2 * h + 2, :],
                in0=a_pick[:, 2 * h : 2 * h + 2, :].rearrange("p t (c i) -> p c t i", i=4),
                in1=b_pick[:, 2 * h : 2 * h + 2, :].rearrange("p t (c i) -> p c t i", i=4),
                op=MAX,
            )
        h_w = tile("h_w", [P, O], U32)
        h_s = tile("h_s", [P, O], U8)
        nc.vector.quantize_mx(out=h_w[:].bitcast(E4X4), scales=h_s[:], in_=hid[:])

        res = [tile("res%d" % h, [P, O], F32) for h in range(2)]
        for h in range(2):
            nc.tensor.matmul_mx(
                out=y[h][:],
                lhsT=wb_w[:, 2 * P * h : 2 * P * (h + 1)].bitcast(E2X4),
                lhsT_scale=c_s[:, P * h : P * (h + 1)],
                rhs=h_w[:].bitcast(E4X4),
                rhs_scale=h_s[:],
                start=False,
                stop=True,
            )
        nc.vector.tensor_copy(out=res[0][:], in_=y[0][:])
        nc.scalar.copy(out=res[1][:], in_=y[1][:])
        nc.sync.dma_start(out=out[0:P, :], in_=res[0][:])
        nc.scalar.dma_start(out=out[P : 2 * P, :], in_=res[1][:])
